import numpy as np, ml_dtypes
CORES = [2,3,42,43,82,83,122,123]
N = 8
BF = ml_dtypes.bfloat16
M, L, CAP, VI, ST = 3072, 256, 128, 4, 3
W = M + (VI - 1) * L
def weights(rng):
    w = rng.integers(0, 64, (N, 8, 16)); o = np.argsort(rng.random((N, 8, 16)), axis=-1)
    a = o[..., :1] == np.arange(16); b = o[..., 1:2] == np.arange(16)
    return np.where(a, 1, np.where(b, 16, w)), a[:, :, None], b[:, :, None]
def aim(v, w, a, b, t):
    v = np.where(a | b, 0, v); need = (t - np.sum(v * w[:, :, None], axis=-1)) & 63
    return v + a * (need & 15)[..., None] + b * (need >> 4)[..., None]
def shake(rng, v, k, top):
    return np.clip(v + np.floor((2 * k + 1) * rng.random(v.shape)).astype(np.int64) - k, 0, top)
def homes(rng, e):
    t = (64 * rng.random((N, 8, M)) ** e).astype(np.int64)
    t = (t * (2 * rng.integers(0, 32, (N, 8, 1)) + 1) + rng.integers(0, 64, (N, 8, 1))) & 63
    t[:, :, 1:65] = np.arange(64); return t
def points(rng, w, a, b, top):
    tree = homes(rng, rng.choice(np.array([1.0, 1.5, 2.0, 3.0]), (N, 8, 1)))
    mid = rng.integers(0, top + 1, (N, 8, 64, 16)); k = rng.integers(0, 9, (N, 8, M, 1)); k[:, :, 1:65] = 0
    v = shake(rng, np.take_along_axis(mid, tree[..., None], 2), k, top)
    far = rng.random((N, 8, M, 1)) < 0.3; far[:, :, 1:65] = False
    return tree, aim(np.where(far, rng.integers(0, top + 1, v.shape), v), w, a, b, tree)
def grow(v, tree):
    x = v.astype(np.int32); c = np.zeros(N * 8 * M * 16, np.int64)
    R, g, n = np.nonzero(np.broadcast_to(np.arange(M) > 64, (N, 8, M))); at = tree[R, g, n] + 1
    for _ in range(24):
        if len(n) == 0: break
        band = np.add.reduce(np.abs(x[R, g, n] - x[R, g, at]), axis=-1) >> 4
        key = ((R * 8 + g) * M + at) * 16 + band
        u, i = np.unique(key, return_index=True); c[u] = n[i]
        more = np.ones(len(n), bool); more[i] = False
        R, g, n, at = R[more], g[more], n[more], c[key[more]]
    return c.reshape(N, 8, M, 16)
def queries(rng, v, tree, w, a, b):
    o = rng.integers(1, M, (N, 8, VI * L)); k = rng.integers(0, 7, (N, 8, VI * L, 1))
    s = shake(rng, np.take_along_axis(v, o[..., None], 2), k, 15)
    s = np.where(rng.random((N, 8, VI * L, 1)) < 0.25, rng.integers(0, 16, s.shape), s)
    return aim(s, w, a, b, np.take_along_axis(tree, o, 2))
def radii(rng):
    z = (N, 8, VI * L)
    return np.where(rng.random(z) < 0.7, rng.integers(100, 256, z), rng.integers(0, 100, z))
def full(v):
    return np.ascontiguousarray(v.transpose(0, 1, 3, 2)).reshape(N, 128, -1)
def pack(v, c, s, w, r0, th):
    return {"pt": full(v).astype(np.float32).astype(BF), "ch": full(c).astype(np.int32), "q": full(s).astype(np.float32).astype(BF),
            "w": np.ascontiguousarray(w.reshape(N, 128, 1)).astype(np.int32), "r0": r0.astype(np.int32), "th": np.repeat(th, 16, axis=1)[..., None].astype(np.int32)}
def setup_inputs(rng):
    w, a, b = weights(rng); tree, v = points(rng, w, a, b, 15)
    return pack(v, grow(v, tree), queries(rng, v, tree, w, a, b), w, radii(rng), rng.integers(20, 60, (N, 8)))
def setup_inputs_room(rng):
    w, a, b = weights(rng); tree, v = points(rng, w, a, b, 10); z = (N, 8, VI * L)
    n = rng.choice(np.array([0, 1, CAP - 1, CAP, CAP + 1, L]), (N, 8)); n[0] = (CAP, CAP + 1, L, CAP - 1, 1, 0, CAP, CAP + 1); n[:, 2] = L
    n = np.concatenate([n[:, :, None], np.full((N, 8, VI - 1), L // 2)], axis=2)
    hot = (np.argsort(rng.random((N, 8, VI, L)), axis=-1) < n[..., None]).reshape(z)
    s = np.where(hot[..., None], rng.integers(12, 16, z + (16,)), queries(rng, v, tree, w, a, b))
    r0 = np.where(hot, rng.choice(np.array([20, 21, 255, 255, 255]), z), rng.integers(0, 20, z))
    return pack(v, grow(v, tree), s, w, r0, np.full((N, 8), 20))
def setup_inputs_knots(rng):
    w, a, b = weights(rng); v = rng.integers(0, 16, (N, 8, M, 16)); v[:, 1::2] = v[:, 1::2][:, :, rng.integers(0, 37, M)]
    dens = rng.choice(np.array([1.0, 0.6, 0.2]), (N, 8, 1, 1)); dens[:, 0] = 1.0; dens[:, 1] = 0.2; dens[:, 2] = 0.3
    c = np.where(rng.random((N, 8, M, 16)) < dens, rng.integers(1, M, (N, 8, M, 16)), 0)
    c[:, 3] = rng.choice(np.array([0, 1, 64, 65, M - 1]), (N, M, 16))
    c[:, 5] = np.where(rng.random((N, M, 16)) < 0.5, np.arange(M)[:, None], c[:, 5])
    x = rng.integers(1, M, (N, M, 2)); e = np.arange(16) - rng.integers(1, 6, (N, M, 1)); j = rng.choice(np.array([-1, 3, 4]), (N, M, 1))
    some = rng.random((N, M, 1)) < 0.4; some[:, 1:65] = True
    c[:, 6] = some * np.where((e >= 0) & (e < 3), x[:, :, :1], np.where(e == j, x[:, :, 1:], 0)); c[:, :, 0] = 0
    return pack(v, c, queries(rng, v, rng.integers(0, 64, (N, 8, M)), w, a, b), w, radii(rng), rng.integers(20, 80, (N, 8)))
def setup_inputs_ties(rng):
    w = rng.integers(0, 64, (N, 8, 16)); v = 4 * rng.integers(0, 4, (N, 8, M, 16)); tree = homes(rng, 1.0); z = (N, 8, VI * L)
    s = np.take_along_axis(v, rng.integers(1, M, z)[..., None], 2); s = np.where(rng.random(s.shape) < 0.3, 4 * rng.integers(0, 4, s.shape), s)
    s = np.where(rng.random(s.shape) < 0.01, 15, s); s[:, ::2, 1::2] = s[:, ::2, ::2]
    r0 = np.where(rng.random(z) < 0.4, 16 * rng.integers(3, 9, z) + rng.choice(np.array([-1, 1]), z), 4 * rng.integers(10, 40, z))
    return pack(v, grow(v, tree), s, w, r0, 4 * rng.integers(8, 15, (N, 8)))
def setup_inputs_ends(rng):
    w, a, b = weights(rng); tree, v = points(rng, w, a, b, 15); n = np.arange(L)
    v[:, 4, 65:65 + L] = rng.integers(0, 16, (N, L, 16)); tree[:, 4, 65:65 + L] = n & 63; v = aim(v, w, a, b, tree)
    s = queries(rng, v, tree, w, a, b); s[:, 4, :L] = v[:, 4, 65:65 + L]
    w[:, 1] = 0; w[:, 2] = 63; v[:, :, 1] = 0; v[:, :, 64] = 15; v[:, :, M - 1] = 15; v[:, 3, 1:65] = 0
    c = grow(v, tree); c[:, :, 1, 15] = M - 1; c[:, 3] = 0; c[:, 4, 65:] = 0; c[:, 4, 1 + (n & 63), 4 * (n >> 6) + 2] = 65 + n
    R = np.arange(N); z = 1 + ((15 * np.sum(w[:, 7], axis=-1)) & 63)
    v[R, 7, z] = 0; v[:, 7, 65] = 0; v[:, 7, 66] = 15
    c[R, 7, z] = 0; c[R, 7, z, 9] = 65; c[:, 7, 65] = 0; c[:, 7, 65, 4] = 66
    s[:, 1, ::3] = 15; s[:, 3, ::2] = 15; s[:, 3, 1::4] = rng.integers(14, 16, s[:, 3, 1::4].shape); s[:, 7, ::4] = 15
    s[:, :, 0] = 15; s[:, :, L - 1] = 0
    r0 = rng.choice(np.array([0, 1, 15, 16, 17, 120, 254, 255]), (N, 8, VI * L)); high = np.array([240, 241, 255])
    r0[:, 3, ::2] = rng.choice(high, r0[:, 3, ::2].shape); r0[:, 3, 1::4] = rng.choice(np.array([191, 192, 239, 240, 241, 255]), r0[:, 3, 1::4].shape)
    r0[:, 4, :L] = 255; r0[:, 7, ::4] = rng.choice(high, r0[:, 7, ::4].shape); r0[:, :, 0] = 255; r0[:, :, L - 1] = 255
    th = rng.choice(np.array([0, 1, 16, 30, 240]), (N, 8)); th[:, 0] = 0; th[:, 3] = np.array([0, 240, 241, 255])[R & 3]; th[:, 4] = 0; th[:, 5] = 255; th[:, 6] = 240
    return pack(v, c, s, w, r0, th)
def setup_inputs_spread(rng):
    w = rng.integers(0, 64, (N, 8, 16)); e = rng.choice(np.array([0.25, 0.5, 1.0, 2.0, 4.0]), (N, 8, 1, 16))
    v = (16 * rng.random((N, 8, M, 16)) ** e).astype(np.int64); s = (16 * rng.random((N, 8, VI * L, 16)) ** e).astype(np.int64)
    c = grow(v, homes(rng, 4.0)); c = np.where(rng.random(c.shape) < 0.1, rng.integers(0, M, c.shape), c); c[:, :, 0] = 0
    th = np.exp2(7 * rng.random((N, 8))).astype(np.int64); th[:, 0] = 8
    return pack(np.clip(v, 0, 15), c, np.clip(s, 0, 15), w, rng.integers(0, 256, (N, 8, VI * L)), th)
def check_inputs(d):
    bad = []
    for k in ("pt", "q"):
        x = np.asarray(d[k]).astype(np.float32)
        if not (np.all(x >= 0) and np.all(x <= 15) and np.all(x == np.floor(x))): bad.append("whole numbers from 0 to 15 in " + k)
    for k, hi in (("ch", M - 1), ("w", 63), ("r0", 255), ("th", 255)):
        if np.min(d[k]) < 0 or np.max(d[k]) > hi: bad.append("range of " + k)
    if np.any(np.asarray(d["ch"])[:, :, 0] != 0): bad.append("column 0 of ch")
    x = np.asarray(d["th"]).reshape(-1, 16)
    if np.any(x != x[:, :1]): bad.append("one threshold a group")
    return bad
def dist(u, v):
    return np.add.reduce(np.abs(u - v), axis=-1)
def inside(D, rho):
    i = np.arange(16); return (16 * i <= (D + rho)[..., None]) & (16 * i + 15 >= (D - rho)[..., None])
def at(k, i):
    return np.take_along_axis(k, i[..., None], -1)[..., 0]
def reference(pt, ch, q, w, r0, th):
    X = np.zeros((N, 8, W, 16), np.int32); X[:, :, :M] = pt.astype(np.float32).astype(np.int32).reshape(N, 8, 16, M).transpose(0, 1, 3, 2)
    C = np.zeros((N, 8, W, 16), np.int32); C[:, :, :M] = ch.reshape(N, 8, 16, M).transpose(0, 1, 3, 2)
    Q = np.ascontiguousarray(q.astype(np.float32).astype(np.int32).reshape(N, 8, 16, VI * L).transpose(0, 1, 3, 2))
    wt = w.astype(np.int32).reshape(N, 8, 1, 16); lim = th.reshape(N, 8, 16)[:, :, :1]
    a, b, ln = np.ogrid[0:N, 0:8, 0:L]; far_off = 1000
    yr, yb, yp, held = [], [], [], None
    for t in range(VI):
        v = np.array(Q[:, :, t * L:(t + 1) * L]); rho = np.array(r0[:, :, t * L:(t + 1) * L]).astype(np.int32); best = np.zeros((N, 8, L), np.int32)
        if held is not None:
            hv, hr, hb, sent, place = held; h = np.nonzero(sent); to = ((h[0] + 1) % N, h[1], place[h])
            v[to] = hv[h]; rho[to] = hr[h]; best[to] = hb[h]
        kid = np.zeros((N, 8, ST + 1, L, 16), np.int32); far = np.zeros((N, 8, ST + 1, L, 16), np.int32); own = np.zeros((N, 8, ST + 1, L), np.int32)
        lev = np.zeros((N, 8, L), np.int64); push = np.ones((N, 8, L), bool)
        m = 1 + (np.add.reduce(wt * v, axis=-1) & 63); D = dist(X[a, b, m], v)
        for s in range(ST + 1):
            if s > 0:
                k = kid[a, b, lev, ln]; f = far[a, b, lev, ln]; ok = (k > 0) & inside(own[a, b, lev, ln], rho)
                i = np.argmin(np.where(ok, f, far_off), axis=-1); push = np.any(ok, axis=-1)
                m = np.where(push, at(k, i), 0); D = np.where(push, at(f, i), far_off)
                h = np.nonzero(push); kid[h[0], h[1], lev[h], h[2], i[h]] = 0
                lev = np.where(push, lev + 1, np.maximum(lev - 1, 0))
            P = np.where(inside(D, rho) & push[..., None], C[a, b, m], 0)
            F = dist(X[a[..., None], b[..., None], P], v[:, :, :, None])
            h = np.nonzero(push); e = (h[0], h[1], lev[h], h[2])
            kid[e] = P[h]; far[e] = F[h]; own[e] = D[h]
            key = np.concatenate([D[..., None], np.where(P > 0, F, far_off)], axis=-1); node = np.concatenate([m[..., None], P], axis=-1)
            i = np.argmin(key, axis=-1); least = at(key, i); better = least < rho
            best = np.where(better, 4096 * a + at(node, i), best); rho = np.where(better, least, rho)
        yr.append(rho); yb.append(best)
        if t == VI - 1: break
        goes = rho >= lim; here = (best > 0) & (best >> 12 == a); node = np.where(here, best & 4095, 0); row = rho >> 4
        can = goes & here & (C[a, b, node, row] == 0)
        earlier = np.arange(L)[None, :] < np.arange(L)[:, None]
        win = can & ~np.any((node[:, :, :, None] == node[:, :, None, :]) & can[:, :, None, :] & earlier, axis=-1)
        X[:, :, M + t * L:M + (t + 1) * L] = v; h = np.nonzero(win); C[h[0], h[1], node[h], row[h]] = M + t * L + h[2]
        yp.append(np.where(win, node, 0))
        place = np.add.accumulate(goes.astype(np.int64), axis=2) - 1
        held = (v, rho, best, goes & (place < CAP), place)
    return {"yr": np.concatenate(yr, axis=2).astype(np.float32), "yb": np.concatenate(yb, axis=2).astype(np.float32), "yp": np.concatenate(yp, axis=2).astype(np.float32)}

from concourse.mybir import AluOpType, AxisListType, ActivationFunctionType

OP = AluOpType
AF = ActivationFunctionType
M0, LN, VI, W = 3072, 256, 4, 3840
C0 = 491520
BIG = 16777216
FR = 1.0 / BIG
TR = 256
CHUNKS = ((32, "S"), (32, "V"), (32, "V"), (32, "V"))

AR = {"af": ("float32", 15800), "ab": ("bfloat16", 35000), "ai": ("int32", 3600), "au": ("uint16", 1200)}
SCRATCH = {k: ("sbuf", [128, n], d) for k, (d, n) in AR.items()}
SCRATCH["ptab"] = ("sbuf", [128, W], "bfloat16")
SCRATCH["ctab"] = ("sbuf", [128, TR + W], "float32")
SCRATCH["cint"] = ("sbuf", [128, M0], "int32")
SCRATCH["qsb"] = ("sbuf", [128, VI * LN], "bfloat16")
for _h in range(2):
    for _b in ("key", "dif", "msc", "lst"):
        SCRATCH["%s%d" % (_b, _h)] = ("psum", [128, 512], "float32")
NY = 40
SEMAPHORES = ["sV", "sS", "sP", "sG"] + ["y%d" % k for k in range(NY)] + ["pq1", "pq2", "pq3", "pr1", "pr2", "pr3", "aq1", "aq2", "aq3", "ar1", "ar2", "ar3"] + ["l%d" % k for k in range(12)]
CYC = 0.83
GX = 1.55
A_SPREAD = "G"
LEAD = 0.0
LOOK = 70.0
LATER = 2500.0
HOP = 90.0


def rank_program(g, core, T, topo):
    rank = T.rank_of(core)
    if rank is None:
        return
    N = len(T.cores)
    ops = []
    acc = {}
    fill = {k: 0 for k in AR}
    names = {}
    bonus = [0.0]
    psum = {k for k in SCRATCH if SCRATCH[k][0] == "psum"}

    def al(name, n, kind):
        n2 = (n + 15) // 16 * 16
        b = fill[kind]
        fill[kind] = b + n2
        if fill[kind] > AR[kind][1]:
            raise ValueError("arena %s" % kind)
        names[name] = (kind, b, n)
        return name

    def v(name, lo=0, hi=None, st=1, p=128):
        if name in names:
            k, b, n = names[name]
        else:
            k, b, n = name, 0, SCRATCH[name][1][1]
        if hi is None:
            hi = n
        return (k, b + lo, b + hi, st, p)

    def ap(x):
        if len(x) == 2:
            return ap(x[0]).indirect(ap(x[1]))
        k, lo, hi, st, p = x
        t = T[k]
        if st == 1:
            return t[0:p, lo:hi]
        return t[0:p, lo:hi:st]

    def width(x):
        if len(x) == 2:
            return 16 * (x[1][2] - x[1][1])
        return len(range(x[1], x[2], x[3]))

    def is2(x):
        return len(x) == 5 and (x[0] in ("ab", "au", "ptab", "qsb"))

    def overlap(a, b):
        if a[1] >= b[2] or b[1] >= a[2]:
            return False
        if a[3] == b[3] and a[3] > 1 and (a[1] - b[1]) % a[3]:
            return False
        return True

    def covers(a, b):
        return (a[3] == 1 and a[1] <= b[1] and a[2] >= b[2]) or a[1:4] == b[1:4]

    def add(eng, emit, reads, writes, busy, lat=0.0, sem=None, extra=()):
        i = len(ops)
        deps = {}

        def dep(j, kind):
            if j == i:
                return
            need = not (eng == "P" and ops[j]["eng"] == "P")
            deps[j] = deps.get(j, False) or need
        flat = []
        for x in reads:
            flat += list(x) if len(x) == 2 else [x]
        wr = []
        for x in writes:
            if len(x) == 2:
                wr.append(x[0])
                flat.append(x[1])
            else:
                wr.append(x)

        def norm(x):
            return (x[0], 0, 512, 1, 128) if x[0] in psum else x
        flat = [norm(x) for x in flat]
        wr = [norm(x) for x in wr]
        for x in flat:
            for (j, y, w) in acc.get(x[0], []):
                if w and overlap(x, y):
                    dep(j, "RAW")
                elif not w and x[0] in psum and ops[j]["eng"] != eng:
                    dep(j, "RR")
        for x in wr:
            for (j, y, w) in acc.get(x[0], []):
                if overlap(x, y):
                    dep(j, "WAW" if w else "WAR")
        for x in flat:
            acc.setdefault(x[0], []).append((i, x, False))
        for x in wr:
            acc[x[0]] = [e for e in acc.get(x[0], []) if e[0] == i or not covers(x, e[1])]
            acc[x[0]].append((i, x, True))
        ops.append({"eng": eng, "emit": emit, "deps": deps, "busy": busy, "lat": lat, "sem": sem, "tdeps": list(extra), "bonus": bonus[0]})
        return i

    def vdur(out, ins, two=False):
        n = width(out)
        for x in ins:
            if len(x) == 2:
                return 50 + GX * CYC * n
        if len(out) == 2:
            return 50 + 3.5 * CYC * width(out)
        c = 1.0
        if two and all(x[0] not in psum for x in ins):
            c = 2.0
        elif not two and is2(out) and all(is2(x) for x in ins):
            c = 0.5
        return 25 + CYC * max(64, c * n)

    def cp(out, a):
        add("V", lambda: g.vector.tensor_copy(ap(out), ap(a)), [a], [out], vdur(out, [a]))

    def tt(out, a, b, op):
        add("V", lambda: g.vector.tensor_tensor(ap(out), ap(a), ap(b), op), [a, b], [out], vdur(out, [a, b], True))

    def ts(out, a, s1, op0, s2=None, op1=None):
        rd = [a] + ([s1] if isinstance(s1, tuple) else [])

        def emit():
            s = ap(s1) if isinstance(s1, tuple) else s1
            if op1 is None:
                return g.vector.tensor_scalar(ap(out), ap(a), s, None, op0)
            return g.vector.tensor_scalar(ap(out), ap(a), s, s2, op0, op1)
        add("V", emit, rd, [out], vdur(out, [a]))

    def scan(out, d0, d1, init, op0, op1):
        add("V", lambda: g.vector.tensor_tensor_scan(ap(out), ap(d0), ap(d1), init, op0, op1), [d0, d1], [out], 25 + CYC * width(out))

    def red(out, a):
        add("V", lambda: g.vector.tensor_reduce(ap(out), ap(a), axis=AxisListType.X, op=OP.min, apply_absolute_value=True), [a], [out], 25 + CYC * width(a))

    def ms(out, c):
        add("V", lambda: g.vector.memset(ap(out), c), [], [out], 25 + CYC * max(64, width(out) * (0.5 if is2(out) else 1)))

    def act(out, a, func, bias=None, scale=None, accum=None):
        rd = [a] + ([bias] if isinstance(bias, tuple) else [])

        def emit():
            kw = {}
            if bias is not None:
                kw["bias"] = ap(bias) if isinstance(bias, tuple) else bias
            if scale is not None:
                kw["scale"] = scale
            if accum is not None:
                kw["accum_out"] = ap(accum)
            return g.scalar.activation(ap(out), ap(a), func, **kw)
        d = 65 + CYC * width(out) * (GX if len(a) == 2 else 1)
        add("S", emit, rd, [out] + ([] if accum is None else [accum]), d + (0 if accum is None else 25))

    def mm(out, parts, start=True, stop=True, outs=None):
        n = len(parts)
        dur = 0.0
        rd = []
        for (a, b) in parts:
            rd += [a, b]
            f = 4 if a[0] == "af" else 1
            dur += 0.72 * f * max(min(64, width(a)), width(b))

        def emit():
            ins = None
            for k, (a, b) in enumerate(parts):
                o = out if outs is None else outs[k]
                ins = g.tensor.matmul(ap(o), ap(a), ap(b), start and k == 0, stop and k == n - 1)
            return ins
        add("P", emit, rd, [out], dur + 30)

    def iota(out, pat, base, cm, fl=False):
        add("G", lambda: g.iota(ap(out), pat, base, cm, allow_small_or_imprecise_dtypes=True) if fl else g.iota(ap(out), pat, base, cm), [], [out], 130 + 2 * CYC * width(out))

    def asel(out, a, pat, cop, fillv, base, cm):
        add("G", lambda: g.affine_select(ap(out), ap(a), pat, cop, fillv, base, cm), [a], [out], 170 + 2 * CYC * width(out))

    ysem = [0]

    def dma(out_fn, in_fn, reads, writes, lat):
        s = "y%d" % ysem[0]
        ysem[0] += 1
        return add("Y", lambda: g.sync.dma_start(out_fn(), in_fn()), reads, writes, 60.0, lat, (s, 16))

    lsem = [0]
    right, left = T.cores[(rank + 1) % N], T.cores[(rank - 1) % N]

    def engs(a, b):
        return topo.engines(a, b)[:8]

    def send(out, a, dst, rsem):
        s = "l%d" % lsem[0]
        lsem[0] += 1
        es = engs(core, dst)
        mk = sum(1 << e for e in es)
        rid, pid = topo.addr(dst)[:2]
        return add("G", lambda: (g.remote_dma(ap(out), ap(a), T.sem[rsem], T.sem[s], pid, rid, mk), None)[1], [a], [], 900.0, 0.0, (s, len(es)))

    def arrive(out, src, rsem, after, lat):
        n = len(engs(src, core))
        return add("R", None, [], [out], 0.0, lat, (rsem, n), [after])

    F, B, I, U = "af", "ab", "ai", "au"
    al("wi", 1, I)
    al("thi", 1, I)
    al("r0i", 1024, I)
    dma(lambda: ap(v("wi")), lambda: T.w[:], [], [v("wi")], 2000)
    dma(lambda: ap(v("qsb")), lambda: T.q[:], [], [v("qsb")], 3000)
    dma(lambda: ap(v("r0i", p=8)), lambda: T.r0[:], [], [v("r0i")], 3200)
    dma(lambda: ap(v("thi")), lambda: T.th[:], [], [v("thi")], 3300)
    dma(lambda: ap(v("ptab", 0, M0)), lambda: T.pt[:], [], [v("ptab", 0, M0)], 5500)
    for k in range(3):
        dma(lambda k=k: ap(v("cint", 1024 * k, 1024 * k + 1024)), lambda k=k: T.ch[:, 1024 * k:1024 * k + 1024], [], [v("cint", 1024 * k, 1024 * k + 1024)], 7000 + 1500 * k)
    ms(v("ptab", M0, W), 0.0)
    ms(v("ctab", TR + M0, TR + W), 0.0)

    for nm, n, k in [("onesb", 128, B), ("onesf", 128, F), ("Ib", 128, B), ("If", 128, F), ("nI", 128, B), ("tri", 128, B),
                     ("TriD", 128, B), ("t8k", 128, B), ("tri8", 128, B), ("dgl", 128, B), ("Blk", 128, B), ("maskL", 128, F), ("rhsC", 8, F), ("BS", 8, B),
                     ("iT", 128, F), ("addR", 128, F), ("mulR", 128, F), ("maxR", 128, F), ("trs", 16, F), ("trw", 16, F), ("zk", 128, B), ("zk0", 128, F), ("zk1", 128, F),
                     ("RS", 8, F), ("RB1", 8, F), ("RTb", 8, B), ("sel", 128, F), ("rowc", 1, F), ("pf", 1, F), ("wf", 1, F), ("thf", 1, F), ("thr", 128, B),
                     ("thv", 8, F), ("WS", 8, B), ("WB", 143, B), ("r0f", 1024, F), ("r0row", 1024, F), ("selg", 2048, B), ("nsel", 1024, B),
                     ("i1", 128, I), ("i2", 128, I), ("i3", 8, I), ("i4", 8, I), ("i5", 128, I), ("i6", 128, I), ("i8", 1, I), ("i9", 1, I),
                     ("zs", 2048, B), ("sg1", 2048, B), ("ns1", 1024, B), ("ic", 128, I), ("id", 128, F), ("il", 80, I), ("lists", 80, U)]:
        al(nm, n, k)
    for t in range(3):
        for h in range(2):
            al("Ik%d%d" % (t, h), 128, B)
    ms(v("onesb"), 1.0)
    ms(v("onesf"), 1.0)
    asel(v("If"), v("onesf"), [[-1, 128]], OP.is_equal, 0.0, 0, 1)
    cp(v("Ib"), v("If"))
    ts(v("nI"), v("Ib"), -1.0, OP.mult)
    cp(v("wf"), v("wi"))
    iota(v("i3"), [[-16, 8]], 0, 1)
    ts(v("i4"), v("i3"), 4, OP.arith_shift_right)
    ts(v("rhsC"), v("i4"), 0.0, OP.is_equal)
    ts(v("WS"), v("rhsC"), v("wf"), OP.mult)
    ms(v("WB"), 0.0)
    cp(v("WB", 15, 128, 16), v("WS"))
    ts(v("BS"), v("rhsC"), 1.0 / 256, OP.mult)
    ts(v("RS"), v("i3"), 0.0, OP.is_equal, 1.0 / 256, OP.mult)
    ts(v("RTb"), v("i3"), 0.0, OP.is_equal)
    ts(v("RB1"), v("i3"), 1.0, OP.is_equal)
    iota(v("il", 0, 8), [[1, 8]], 0, 0)
    iota(v("il", 8, 16), [[16, 8]], 15, 0)
    for k in range(6):
        iota(v("il", 16 + 8 * k, 24 + 8 * k), [[7, 8]], 1 + k, 0)
    cp(v("lists", 0, 64), v("il", 0, 64))

    def lst(k):
        return v("lists", 8 * k, 8 * k + 8)
    iota(v("i1"), [[-1, 128]], 256, 1)
    ts(v("i2"), v("i1"), 15, OP.bitwise_and)
    ts(v("maskL"), v("i2"), 0.0, OP.is_equal)
    iota(v("i5"), [[-16, 8], [0, 16]], 0, 1)
    ts(v("i6"), v("i5"), 4, OP.arith_shift_right)
    ts(v("Blk"), v("i6"), 0.0, OP.is_equal)
    iota(v("iT"), [[0, 8], [1, 16]], 0, 0, True)
    ts(v("addR"), v("iT"), 0.0, OP.is_equal, 4.0, OP.mult)
    ts(v("maxR"), v("iT"), 0.0, OP.is_equal)
    ts(v("mulR"), v("iT"), 0.0, OP.is_gt)
    ts(v("zk0"), v("iT"), -16.0, OP.mult)
    asel(v("zk1", p=2), v("zk0", p=2), [[0, 128]], OP.is_ge, -7.5, 0, -1)
    cp(v("zk", p=2), v("zk1", p=2))
    iota(v("i8"), [[0, 1]], 0, 1)
    cp(v("pf"), v("i8"))
    ts(v("i9"), v("i8"), 15, OP.bitwise_and)
    ts(v("rowc"), v("i9"), 4096.0 * FR, OP.mult, C0 * FR, OP.add)
    iota(v("ic", p=16), [[1, 128]], 0, -16)
    ts(v("sel", p=16), v("ic", p=16), 0.0, OP.is_equal)
    ts(v("id", p=16), v("ic", p=16), -127.0, OP.is_equal)
    tt(v("sel", p=16), v("sel", p=16), v("id", p=16), OP.add)
    cp(v("r0f", p=8), v("r0i", p=8))
    for k in range(2):
        mm(v("dif%d" % k), [(v("sel", p=8), v("r0f", 512 * k, 512 * k + 512, p=8))])
        act(v("r0row", 512 * k, 512 * k + 512), v("dif%d" % k), AF.Copy)
    for t in range(1, 4):
        al("hq%d" % t, 512, B)
        al("hr%d" % t, 512, F)
        al("lq%d" % t, 128, B)
        al("lr%d" % t, 128, F)
    for t in range(1, 4):
        j = send(v("hq%d" % t, 0, 128), v("qsb", 256 * t, 256 * t + 128), left, "pq%d" % t)
        arrive(v("hq%d" % t, 0, 128), right, "pq%d" % t, j, 6000.0)
        j = send(v("hr%d" % t, 0, 128), v("r0row", 256 * t, 256 * t + 128), left, "pr%d" % t)
        arrive(v("hr%d" % t, 0, 128), right, "pr%d" % t, j, 6000.0)
    ms(v("ptab", 0, 1), 31.0)
    for k in range(3):
        cp(v("ctab", TR + 1024 * k, TR + 1024 * k + 1024), v("cint", 1024 * k, 1024 * k + 1024))
    asel(v("tri"), v("onesb"), [[1, 128]], OP.is_gt, 0.0, 0, -1)
    ts(v("TriD"), v("Ib"), -1024.0, OP.mult)
    tt(v("TriD"), v("TriD"), v("tri"), OP.add)
    ms(v("t8k"), 8192.0)
    asel(v("tri8"), v("t8k"), [[1, 128]], OP.is_ge, 0.0, 0, -1)
    ts(v("dgl"), v("Ib"), v("pf"), OP.mult)
    for t in range(3):
        for h in range(2):
            ts(v("Ik%d%d" % (t, h)), v("Ib"), float(M0 + 256 * t + 128 * h), OP.mult)
    iota(v("trs"), [[128, 2], [0, 8]], 256 - 1024, 1, True)
    iota(v("trw"), [[128, 2], [0, 8]], 0, 1, True)
    cp(v("thf"), v("thi"))
    ts(v("thr"), v("onesf"), v("thf"), OP.mult)
    mm(v("lst0", 0, 8), [(v("thr"), v("RTb"))])
    ts(v("thv"), v("lst0", 0, 8), 1.0 / 256, OP.mult, C0 * FR, OP.add)
    ms(v("zs", p=16), 0.0)
    asel(v("sg1", p=16), v("zs", p=16), [[-1, 8], [0, 256]], OP.not_equal, 1.0, 0, 1)
    asel(v("selg", p=16), v("sg1", p=16), [[-1, 8], [0, 256]], OP.not_equal, 1.0, -8, 1)
    asel(v("ns1", p=16), v("zs", 0, 1024, p=16), [[-1, 8], [0, 128]], OP.not_equal, -1.0, 0, 1)
    asel(v("nsel", p=16), v("ns1", p=16), [[-1, 8], [0, 128]], OP.not_equal, -1.0, -8, 1)

    for h in range(2):
        for nm, n, k in [("P16", 128, U), ("mo", 8, U), ("kS", 128, F), ("gm", 128, B), ("adm", 128, B), ("pen", 128, B), ("df", 2048, B),
                         ("ad", 2048, B), ("sc1", 128, F), ("ins", 128, B), ("t1", 8, I), ("mI", 8, I), ("E", 128, F), ("li", 8, I), ("li2", 8, I),
                         ("rm", 8, I), ("rm2", 8, I), ("rm3", 8, F), ("kd", 8, F), ("bi", 8, F), ("np2", 8, F), ("sl0", 8, F), ("sel3", 8, F),
                         ("a3", 128, B), ("b3", 128, B), ("s3", 128, F),
                         ("tI", 56, I), ("H", 56, I), ("L", 56, I), ("upd", 56, F), ("nu", 56, F), ("pk", 56, F), ("nsc", 56, F), ("O", 16, F), ("Og", 128, F),
                         ("nz", 8, F), ("bz", 8, F), ("bb", 8, F), ("cd", 8, F), ("slt", 8, F), ("sl16", 8, U), ("rbs", 128, F), ("bI", 56, I), ("oh", 128, B),
                         ("nb16", 8, U), ("Kb", 128, F), ("pr", 128, F), ("osc", 128, F), ("vals", 128, F), ("nF", 8, I), ("dgi", 16, I), ("z", 8, F), ("nc", 8, F),
                         ("DG", 16, B), ("dm", 8, F), ("sq0", 256, F), ("sq1", 256, F), ("sq2", 256, F), ("sq3", 256, F), ("sr", 256, B),
                         ("nd", 8, F), ("wn", 8, F), ("wg", 128, F), ("z2", 8, F), ("ncs", 8, F), ("z3", 8, F), ("off", 8, F), ("of16", 8, U)]:
            al(nm + str(h), n, k)
        for s in range(4):
            al("As%d%d" % (s, h), 128, F)
        for s in range(3):
            al("v2%d%d" % (s, h), 128, F)
            al("sc2%d%d" % (s, h), 128, F)
        for k in range(2):
            al("NB%d%d" % (k, h), 56, F)
            ms(v("NB%d%d" % (k, h)), 1.5)
        ms(v("nsc%d" % h), 0.0)
    al("FAR", 16, B)
    al("Ud", 256, B)
    al("q16a", 2048, B)
    for t in range(4):
        al("q16b%d" % t, 2048, B)

    def qv(t, h):
        if h == 0 and t > 0:
            return ("lq%d" % t, 0)
        return ("qsb", 256 * t + 128 * h)

    def q16(t, h):
        return "q16a" if h == 0 else "q16b%d" % t

    def spread(t, h, how):
        nm, o = qv(t, h)
        for i in range(16):
            out, a = v(q16(t, h), i, 2048, 16), v(nm, o, o + 128)
            if how == "G":
                asel(out, a, [[0, 128]], OP.is_ge, 0.0, 1, 0)
            elif how == "V" or i % 3 < 2:
                cp(out, a)
            else:
                act(out, a, AF.Copy)

    def tolist(h, win, offs, dst, plus=None):
        E = v("E%d" % h)
        tt(E, (win, offs), v("maskL"), OP.mult)
        o = v("lst%d" % h, 0, 8)
        mm(o, [(E, v("rhsC"))])
        if plus is None:
            cp(dst, o)
        else:
            ts(dst, o, float(plus), OP.add)

    def begin(t, h):
        nm, o = qv(t, h)
        hs = str(h)
        NB = "NB%d%d" % (t % 2, h)
        if t < 3:
            act(v("ptab", M0 + 256 * t + 128 * h, M0 + 256 * t + 128 * h + 128), v(nm, o, o + 128), AF.Copy)
        l8 = v("lst" + hs, 0, 8)
        mm(l8, [(v("WB", 15 - l, 143 - l), v(nm, o + l, o + 128, 16)) for l in range(16)])
        cp(v("li" + hs), l8)
        ts(v("li2" + hs), v("li" + hs), 63, OP.bitwise_and)
        ts(v("mo" + hs), v("li2" + hs), 1.0, OP.add)
        m8 = v("msc" + hs, 0, 8)
        mm(m8, [(v(nm, o, o + 128), v("WS"))])
        cp(v("rm" + hs), m8)
        ts(v("rm2" + hs), v("rm" + hs), 63, OP.bitwise_and)
        ts(v("rm3" + hs), v("rm2" + hs), FR, OP.mult, (1 + C0) * FR, OP.add)
        if h == 0 and t > 0:
            rv = v("lr%d" % t)
        else:
            rv = v("r0row", 256 * t + 128 * h, 256 * t + 128 * h + 128)
        mm(m8, [(rv, v("RS"))])
        ts(v(NB, 1, 56, 7), m8, C0 * FR, OP.add)
        if h == 0 and t > 0:
            mm(m8, [(rv, v("RB1"))])
            cp(v("bi" + hs), m8)

    def push(t, h, s):
        hs = str(h)
        NB = "NB%d%d" % (t % 2, h)
        nm, o = qv(t, h)
        W1 = M0 + 256 * t
        mo = v("mo" + hs)
        ch, pt = v("ctab", TR, TR + W1), v("ptab", 0, W1)
        key = v("key" + hs, 0, 128)
        cp(v("P16" + hs), (ch, mo))
        act(v("gm" + hs), (pt, mo), AF.Copy)
        mz = v("msc" + hs, 0, 128)
        mm(mz, [(v("Ib"), v("gm" + hs)), (v("nI"), v(nm, o, o + 128))])
        act(v("adm" + hs), mz, AF.Abs)
        act(v("kS" + hs), (ch, mo), AF.Identity, bias=v("rowc"), scale=FR)
        As = v("As%d%d" % (s, h))
        if s == 0:
            m2 = v("msc" + hs, 256, 264)
            mm(m2, [(v("adm" + hs), v("BS"))])
            tt(v("kd" + hs), m2, v("rm3" + hs), OP.add)
            tt(v(NB, 2, 56, 7), v("kd" + hs), v(NB, 1, 56, 7), OP.min)
        m3 = v("msc" + hs, 128, 256)
        mm(m3, [(v("adm" + hs), v("Blk")), (v("onesb", p=2), v("zk", p=2))])
        act(As, m3, AF.Abs, scale=1.0 / 256)
        prev = 1 if s == 0 else s + 2
        tt(v("pen" + hs), (v(NB), lst(1 + prev)), As, OP.is_lt)
        mm(key, [(v("kS" + hs), v("If")), (v("Ib"), v("pen" + hs))], True, False)
        l0 = 0
        save = bonus[0]
        for n_l, who in CHUNKS:
            P = v("P16" + hs, l0, l0 + n_l)
            a, b = 16 * l0, 16 * (l0 + n_l)
            l0 += n_l
            df, ad, qq = v("df" + hs, a, b), v("ad" + hs, a, b), v(q16(t, h), a, b)
            bonus[0] = save - LATER
            if who == "S":
                act(df, (pt, P), AF.Copy)
                d = v("dif" + hs, 0, b - a)
                mm(d, [(v("Ib"), df), (v("nI"), qq)])
                act(ad, d, AF.Abs)
            else:
                tt(df, (pt, P), qq, OP.subtract)
                act(ad, df, AF.Abs)
        bonus[0] = save
        mm(key, [(v("ad" + hs, i, 2048, 16), v("BS")) for i in range(16)], False, True, [v("key" + hs, i, 128, 16) for i in range(16)])
        sc1 = "sc1" + hs
        scan(v(sc1), v("addR"), key, 4.0, OP.add, OP.min)
        k15 = v(sc1, 15, 128, 16)
        if s < 3:
            v2, sc2 = v("v2%d%d" % (s, h)), "sc2%d%d" % (s, h)
            if s == 0:
                tt(v(NB, 3, 56, 7), v(NB, 2, 56, 7), k15, OP.min)
                tt(v("ins" + hs), (v(NB), lst(4)), As, OP.is_lt)
            else:
                tt(v("ins" + hs), (v(sc1), lst(1)), As, OP.is_lt)
            tt(v2, key, v("ins" + hs), OP.max)
            scan(v(sc2), v("maxR"), v2, 1.0, OP.max, OP.min)
            src = v(sc2, 15, 128, 16)
            if s == 2:
                tt(v("sel3" + hs), src, v("sl0" + hs), OP.min)
                src = v("sel3" + hs)
            ts(v("t1" + hs), src, float(BIG), OP.mult, -float(C0), OP.add)
            ts(v("mI" + hs), v("t1" + hs), 4095, OP.bitwise_and)
            tolist(h, v("mI" + hs), lst(0), mo)
        if s > 0:
            tt(v(NB, s + 3, 56, 7), v(NB, s + 2, 56, 7), k15, OP.min)
        if s == 1:
            v20, s20 = v("v20" + hs), v("sc20" + hs)
            tt(v("a3" + hs), (s20, lst(1)), v20, OP.is_ge)
            tt(v("b3" + hs), (v(NB), lst(5)), v("As0" + hs), OP.is_lt)
            m4 = v("msc" + hs, 384, 512)
            mm(m4, [(v("If"), v20), (v("Ib"), v("a3" + hs)), (v("Ib"), v("b3" + hs))])
            scan(v("s3" + hs), v("maxR"), m4, 1.0, OP.max, OP.min)
            ts(v("np2" + hs), v("sc21" + hs, 15, 128, 16), 1.0, OP.is_lt)
            tt(v("sl0" + hs), v("np2" + hs), v("s3" + hs, 15, 128, 16), OP.max)

    def finish(t, h):
        hs = str(h)
        NB = "NB%d%d" % (t % 2, h)
        if t < 3:
            tt(v("FAR", 8 * h, 8 * h + 8), v(NB, 6, 56, 7), v("thv"), OP.is_ge)
        ts(v("tI" + hs), v(NB), float(BIG), OP.mult, -float(C0), OP.add)
        ts(v("H" + hs), v("tI" + hs), 16, OP.arith_shift_right)
        ts(v("L" + hs), v("tI" + hs), 4095, OP.bitwise_and)
        tt(v("upd" + hs, 1, 56), v("H" + hs, 1, 56), v("H" + hs, 0, 55), OP.is_lt)
        tt(v("nu" + hs, 1, 56), v("H" + hs, 1, 56), v("H" + hs, 0, 55), OP.is_ge)
        tt(v("pk" + hs, 1, 56), v("upd" + hs, 1, 56), v("L" + hs, 1, 56), OP.mult)
        scan(v("nsc" + hs, 1, 56), v("nu" + hs, 1, 56), v("pk" + hs, 1, 56), 0.0, OP.mult, OP.add)

    def node(h):
        return v("nsc%d" % h, 6, 56, 7)

    def codes(t, h):
        hs = str(h)
        cp(v("O" + hs, 0, 8), v("H" + hs, 6, 56, 7))
        ts(v("nz" + hs), node(h), 0.0, OP.is_gt, float(4096 * rank), OP.mult)
        if h == 0 and t > 0:
            tt(v("cd" + hs), node(h), v("nz" + hs), OP.add)
            ts(v("bz" + hs), node(h), 0.0, OP.is_equal)
            tt(v("bb" + hs), v("bz" + hs), v("bi" + hs), OP.mult)
            tt(v("O" + hs, 8, 16), v("cd" + hs), v("bb" + hs), OP.add)
        else:
            tt(v("O" + hs, 8, 16), node(h), v("nz" + hs), OP.add)
        mm(v("lst" + hs, 0, 128, p=16), [(v("O" + hs), v("If"))])
        act(v("Og" + hs, p=16), v("lst" + hs, 0, 128, p=16), AF.Copy)
        k, b, n = names["Og" + hs]
        c = 256 * t + 128 * h
        dma(lambda: T.yr[:, c:c + 128], lambda: T[k][0:8, b:b + 128], [v("Og" + hs)], [], 2000)
        dma(lambda: T.yb[:, c:c + 128], lambda: T[k][8:16, b:b + 128], [v("Og" + hs)], [], 2000)

    def slots(t, h):
        hs = str(h)
        o = v("lst" + hs, 0, 8)
        parts = [(v("TriD"), v("FAR", 8 * h, 8 * h + 8))]
        if h == 1:
            parts.append((v("onesb"), v("FAR", 0, 8)))
        mm(o, parts)
        tt(v("slt" + hs), o, v("trs", 8 * h, 8 * h + 8), OP.min)
        tolist(h, v("slt" + hs), lst(0), v("sl16" + hs), 1024)
        nm, qo = qv(t, h)
        cp((v("hq%d" % (t + 1)), v("sl16" + hs)), v(nm, qo, qo + 128))

    def radii(t, h):
        hs = str(h)
        m = v("msc" + hs, 0, 128)
        mm(m, [(v("sel", p=16), v("Og" + hs, p=16))])
        act(v("rbs" + hs), m, AF.Copy)
        cp((v("hr%d" % (t + 1)), v("sl16" + hs)), v("rbs" + hs))

    def grow1(t, h):
        hs = str(h)
        tolist(h, v("nsc" + hs), lst(7), v("nb16" + hs))
        act(v("Kb" + hs), (v("ctab", TR, TR + M0 + 256 * t), v("nb16" + hs)), AF.Copy)
        ts(v("bI" + hs), v("tI" + hs), 20, OP.arith_shift_right)
        oh = v("oh" + hs)
        tt(oh, (v("bI" + hs), lst(7)), v("iT"), OP.is_equal)
        m = v("msc" + hs, 0, 128)
        mm(m, [(v("Kb" + hs), v("If"))])
        tt(v("pr" + hs), m, oh, OP.mult)
        scan(v("osc" + hs), v("mulR"), v("pr" + hs), 0.0, OP.mult, OP.add)
        tt(v("nF" + hs), node(h), v("FAR", 8 * h, 8 * h + 8), OP.mult)
        ts(v("dgi" + hs, 0, 8), v("nF" + hs), 4032, OP.bitwise_and)
        ts(v("dgi" + hs, 8, 16), v("nF" + hs), 63, OP.bitwise_and)
        ts(v("z" + hs), v("osc" + hs, 15, 128, 16), 0.0, OP.is_equal)
        tt(v("DG" + hs, 0, 8), v("z" + hs), v("dgi" + hs, 0, 8), OP.mult)
        tt(v("DG" + hs, 8, 16), v("z" + hs), v("dgi" + hs, 8, 16), OP.mult)
        tt(v("nc" + hs), v("z" + hs), v("nF" + hs), OP.mult)
        mm(v("lst" + hs, 0, 128, p=16), [(v("DG" + hs), v("Ib"))])
        act(v("Ud", 128 * h, 128 * h + 128, p=16), v("lst" + hs, 0, 128, p=16), AF.Copy)
        ts(v("z2" + hs), v("nc" + hs), 0.0, OP.is_gt, float(TR), OP.mult)
        tt(v("ncs" + hs), v("z2" + hs), v("nc" + hs), OP.add)
        d = v("msc" + hs, 0, 128)
        mm(d, [(oh, v("dgl")), (oh, v("Ik%d%d" % (t, h))), (v("If"), v("Kb" + hs))])
        act(v("vals" + hs), d, AF.Copy)

    def grow2(t, h):
        hs = str(h)
        w = 128 * (h + 1)
        per = 512 // w
        for b in range(8 // per):
            vec = 2 * b < 8 // per
            bank = ("dif0", "dif1", "key0", "key1")[b if h == 1 else 2 * b]
            gs = range(per * b, per * b + per)
            for k, gg in enumerate(gs):
                x = v(bank, w * k, w * k + w)
                y = v(bank, w * k + w - 128, w * k + w)
                neg = (v("nsel", 128 * gg, 128 * gg + 128, p=16), v("Ud", 0, w, p=16))
                own = (v("Ud", 128 * h, 128 * h + 128, p=16), v("selg", 256 * gg, 256 * gg + w, p=16))
                if vec:
                    mm(x, [own, neg, (v("Ib"), v("tri8"))], True, True, [x, x, y])
                else:
                    mm(x, [neg, (v("Ib"), v("tri8"))], True, True, [x, y])
            for k, gg in enumerate(gs):
                x = v(bank, w * k, w * k + w)
                if vec:
                    red(v("dm" + hs, gg, gg + 1), x)
                else:
                    act(v("sq%d" % (gg % 4) + hs, 0, w), x, AF.Square, bias=v("nc" + hs, gg, gg + 1))
            for gg in gs:
                if not vec:
                    act(v("sr" + hs, 0, w), v("sq%d" % (gg % 4) + hs, 0, w), AF.Relu, bias=1.0, scale=-1.0, accum=v("dm" + hs, gg, gg + 1))
        ts(v("nd" + hs, 0, 4), v("dm" + hs, 0, 4), 0.5, OP.is_gt)
        ts(v("nd" + hs, 4, 8), v("dm" + hs, 4, 8), 0.5, OP.is_lt)
        tt(v("z3" + hs), v("nd" + hs), v("ncs" + hs), OP.mult)
        tt(v("off" + hs), v("z3" + hs), v("trw", 8 * h, 8 * h + 8), OP.max)
        tolist(h, v("off" + hs), lst(0), v("of16" + hs))
        cp((v("ctab"), v("of16" + hs)), v("vals" + hs))
        tt(v("wn" + hs), v("nd" + hs), v("nc" + hs), OP.mult)
        mm(v("lst" + hs, 0, 128, p=8), [(v("wn" + hs), v("If"))])
        act(v("wg" + hs, p=8), v("lst" + hs, 0, 128, p=8), AF.Copy)
        c = 256 * t + 128 * h
        dma(lambda: T.yp[:, c:c + 128], lambda: ap(v("wg" + hs, p=8)), [v("wg" + hs)], [], 2000)

    for h in range(2):
        spread(0, h, "VS")
    for t in range(1, 4):
        spread(t, 1, "G")
    begin(0, 0)
    begin(0, 1)
    for t in range(VI):
        order = (0, 1) if t == 0 else (1, 0)
        for s in range(4):
            for h in order:
                bonus[0] = LEAD * (1 - h)
                push(t, h, s)
        bonus[0] = 0.0
        for h in order:
            finish(t, h)
        if t < 3:
            for h in (0, 1):
                slots(t, h)
            jq = send(v("lq%d" % (t + 1)), v("hq%d" % (t + 1), 0, 128), right, "aq%d" % (t + 1))
            arrive(v("lq%d" % (t + 1)), left, "aq%d" % (t + 1), jq, 3000.0)
        for h in order:
            codes(t, h)
        if t < 3:
            for h in order:
                grow1(t, h)
            for h in (0, 1):
                radii(t, h)
            jr = send(v("lr%d" % (t + 1)), v("hr%d" % (t + 1), 0, 128), right, "ar%d" % (t + 1))
            arrive(v("lr%d" % (t + 1)), left, "ar%d" % (t + 1), jr, 3000.0)
            for h in order:
                grow2(t, h)
            begin(t + 1, 1)
            spread(t + 1, 0, A_SPREAD)
            begin(t + 1, 0)

    n = len(ops)
    succ = [[] for _ in range(n)]
    cnt = [0] * n
    for i, o in enumerate(ops):
        ps = set(o["deps"]) | set(o["tdeps"])
        cnt[i] = len(ps)
        for j in ps:
            succ[j].append(i)
    pri = [0.0] * n
    for i in range(n - 1, -1, -1):
        o = ops[i]
        pri[i] = o["busy"] + o["lat"] + max([pri[k] + HOP for k in succ[i]] + [0.0])
    free = {e: 0.0 for e in "VSPGYR"}
    ready = {e: [] for e in free}
    est = [0.0] * n
    for i in range(n):
        if cnt[i] == 0:
            ready[ops[i]["eng"]].append(i)
    sched = []
    left_n = n
    while left_n:
        bt, be = None, None
        for e in free:
            if ready[e]:
                t0 = max(free[e], min(est[i] for i in ready[e]))
                if bt is None or t0 < bt:
                    bt, be = t0, e
        cand = [i for i in ready[be] if est[i] <= bt + LOOK]
        i = max(cand, key=lambda k: (pri[k] + ops[k]["bonus"], -k))
        ready[be].remove(i)
        o = ops[i]
        sched.append(i)
        left_n -= 1
        bt = max(bt, est[i])
        end = bt + o["busy"]
        if be != "R":
            free[be] = end
        for k in succ[i]:
            need = ops[k]["deps"].get(i, True)
            a = (end + o["lat"] + HOP) if need else end
            est[k] = max(est[k], a)
            cnt[k] -= 1
            if cnt[k] == 0:
                ready[ops[k]["eng"]].append(k)

    queue = {"V": g.vector, "S": g.scalar, "P": g.tensor, "G": g, "Y": g.sync}
    count = {"V": 0, "S": 0, "P": 0, "G": 0}
    known = {e: {} for e in queue}
    done = [None] * n
    clock = [None] * n
    totals = {}
    for i in sched:
        o = ops[i]
        e = o["eng"]
        if e == "R":
            done[i] = (o["sem"][0], o["sem"][1])
            totals[done[i][0]] = done[i][1]
            clock[i] = {done[i][0]: done[i][1]}
            continue
        kn = known[e]
        want = {}
        for j, need in o["deps"].items():
            if need:
                s, val = done[j]
                if kn.get(s, 0) < val and want.get(s, (0, 0))[0] < val:
                    want[s] = (val, j)
        for s in list(want):
            val = want[s][0]
            if any(s2 != s and clock[want[s2][1]].get(s, 0) >= val for s2 in want):
                del want[s]
        for s, (val, j) in want.items():
            queue[e].wait_ge(T.sem[s], val)
            for s2, v2 in clock[j].items():
                if kn.get(s2, 0) < v2:
                    kn[s2] = v2
        ins = o["emit"]()
        if o["sem"] is None:
            count[e] += 1
            s, val = "s" + e, count[e]
            ins.then_inc(T.sem[s], 1)
        else:
            s, val = o["sem"][0], o["sem"][1]
            if e == "Y":
                ins.then_inc(T.sem[s], 16)
        done[i] = (s, val)
        totals[s] = max(totals.get(s, 0), val)
        c = dict(kn)
        c[s] = val
        clock[i] = c
    kn = known["G"]
    for s in totals:
        if kn.get(s, 0) < totals[s]:
            g.wait_ge(T.sem[s], totals[s])
